import numpy as np
import ml_dtypes


def mxq(x, axis, fmt="e4m3"):
    dtype, down = {"e4m3": (ml_dtypes.float8_e4m3fn, 7), "e5m2": (ml_dtypes.float8_e5m2, 14)}[fmt]
    v = np.moveaxis(np.asarray(x, np.float32).astype(ml_dtypes.bfloat16).astype(np.float64), axis, -1)
    blocks = v.reshape(v.shape[:-1] + (-1, 32))
    amax = np.abs(blocks).max(-1, keepdims=True)
    byte = np.maximum(np.where(amax > 0, np.frexp(amax)[1] - 1 + 127, 0) - down, 1)
    scale = np.exp2(byte - 127.0)
    codes = (blocks / scale).astype(np.float32).astype(dtype).astype(np.float64)
    return np.moveaxis((codes * scale).reshape(v.shape), -1, axis)


WIDE = False


def mx_kscale(k):
    if not WIDE:
        return np.ones(k)
    levels = np.array([10, -10, 5, -5, 0])
    if k % 512:
        return np.exp2(np.random.permutation(np.resize(levels, k // 32))).repeat(32)
    a = np.empty((k // 512, 16))
    for p in range(k // 512):
        a[p, :8] = np.random.permutation(np.resize(levels, 8))
        for g in range(8):
            far = levels[np.abs(levels - a[p, g]) >= 10]
            a[p, g + 8] = far[np.random.randint(len(far))]
    return np.exp2(a.ravel()).repeat(32)


def f64(x):
    return np.asarray(x).astype(np.float64)


def striped8(idx):
    return np.asarray(idx).reshape(8, -1, 16).transpose(0, 2, 1).reshape(128, -1).astype(np.uint16)


def unstriped8(offs):
    return offs.reshape(8, 16, -1).transpose(0, 2, 1).reshape(8, -1).astype(np.int64)


def pick8(x, idx, run):
    r = np.arange(len(x))
    return x[r[:, None], idx[r % (8 * run) // run]]


E2M1 = np.array([0.0, 0.5, 1.0, 1.5, 2.0, 3.0, 4.0, 6.0, -0.0, -0.5, -1.0, -1.5, -2.0, -3.0, -4.0, -6.0])


def pack_weight(w, fmt):
    k, n = w.shape
    w = f64(np.asarray(w, np.float32).astype(ml_dtypes.bfloat16)).reshape(k // 32, 32, n)
    amax = np.abs(w).max(1)
    if fmt == "e4m3":
        byte = np.frexp(amax)[1] - 1 + 127 - 7
    else:
        mant, ex = np.frexp(amax / 6.0)
        byte = np.where(mant > 0.5, ex, ex - 1) + 127
    byte = np.clip(np.where(amax > 0, byte, 1), 1, 254)
    scaled = (w * np.exp2(127.0 - byte)[:, None, :]).reshape(k, n).astype(np.float32)
    by_word = np.ascontiguousarray(scaled.reshape(k // 512, 128, 4, n).transpose(0, 1, 3, 2))
    if fmt == "e4m3":
        words = by_word.astype(ml_dtypes.float8_e4m3fn).view(np.uint8)
    else:
        c = by_word.astype(ml_dtypes.float4_e2m1fn).view(np.uint8) & 0xF
        words = (c[..., 0::2] | (c[..., 1::2] << 4)).reshape(k // 512, 128, 2 * n)
    return np.ascontiguousarray(words), np.ascontiguousarray(byte.astype(np.uint8).reshape(k // 512, 16, n))


def unpack_weight(words, scales, fmt):
    g, _, n = scales.shape
    words = np.ascontiguousarray(words).reshape(g, 128, n, -1)
    if fmt == "e4m3":
        vals = words.view(ml_dtypes.float8_e4m3fn).astype(np.float64)
    else:
        nib = np.empty((g, 128, n, 4), np.uint8)
        nib[..., 0::2] = words & 0xF
        nib[..., 1::2] = words >> 4
        vals = E2M1[nib]
    vals = vals * np.repeat(np.exp2(scales.astype(np.float64) - 127.0), 8, axis=1)[..., None]
    return vals.transpose(0, 1, 3, 2).reshape(g * 512, n)


D, T, U, I, Q = 512, 1024, 1024, 512, 128


def setup_inputs():
    n = np.random.standard_normal
    idx = np.stack([np.random.permutation(T)[:I] for _ in range(8)])
    idx2 = np.stack([np.random.permutation(U)[:I] for _ in range(8)])
    idx3 = np.stack([np.random.permutation(T)[:I] for _ in range(8)])
    fd = mx_kscale(D)
    keysp = pack_weight(n((D, T)) / fd[:, None], "e4m3")
    notesp = pack_weight(n((D, U)) / fd[:, None], "e2m1")
    return {
        "query": (n((D, Q)) * 1.0 / np.sqrt(D) * fd[:, None]).astype(np.float32),
        "keys_words": keysp[0],
        "keys_scales": keysp[1],
        "notes_words": notesp[0],
        "notes_scales": notesp[1],
        "offs": striped8(idx),
        "offs2": striped8(idx2),
        "offs3": striped8(idx3),
    }


def reference(query, keys_words, keys_scales, notes_words, notes_scales, offs, offs2, offs3):
    idx = unstriped8(offs)
    idx2 = unstriped8(offs2)
    idx3 = unstriped8(offs3)
    keysu = unpack_weight(keys_words, keys_scales, "e4m3")
    notesu = unpack_weight(notes_words, notes_scales, "e2m1")
    queryq = mxq(f64(query), 0, "e4m3")
    a = queryq.T @ keysu
    b = queryq.T @ notesu
    w = np.maximum(pick8(a, idx, 16), pick8(b, idx2, 16))
    r = w - pick8(a, idx, 16)
    f1 = np.zeros((Q, T))
    f1[np.arange(Q)[:, None], idx[np.arange(Q) % 128 // 16]] = r
    a2 = a + f1
    y = pick8(a2, idx3, 16) - w
    return y

@@ -1,0 +1,137 @@
+from contextlib import ExitStack
+
+import concourse.mybir as mybir
+
+D, T, U, SLOTS, Q = 512, 1024, 1024, 512, 128
+FLOPS = 2 * D * Q * (T + U)
+
+F32 = mybir.dt.float32
+BF16 = mybir.dt.bfloat16
+I32 = mybir.dt.int32
+U32 = mybir.dt.uint32
+U16 = mybir.dt.uint16
+U8 = mybir.dt.uint8
+FP8X4 = mybir.dt.float8_e4m3fn_x4
+FP4X4 = mybir.dt.float4_e2m1fn_x4
+ALU = mybir.AluOpType
+COPY = mybir.ActivationFunctionType.Copy
+
+P = 128
+PACK = 4
+CHUNK = 256
+HALF = SLOTS // 2
+LIST_COLS = SLOTS // 16
+
+
+def load_scale_rows(queue, plane, scales):
+    for quad in range(4):
+        queue.dma_start(
+            out=plane[32 * quad : 32 * quad + 4, :].bitcast(I32),
+            in_=scales[0, 4 * quad : 4 * quad + 4, :].bitcast(I32),
+        )
+
+
+def tile_attend_keptbest_two_kernel(
+    tc, query, keys_words, keys_scales, notes_words, notes_scales, offs, offs2, offs3, out
+):
+    nc = tc.nc
+    with ExitStack() as ctx:
+        sb = ctx.enter_context(tc.tile_pool(name="sb", bufs=1))
+        psum = ctx.enter_context(tc.psum_pool(name="psum", bufs=1))
+
+        idx = sb.tile([P, LIST_COLS], U16, name="idx")
+        idx2 = sb.tile([P, LIST_COLS], U16, name="idx2")
+        idx3 = sb.tile([P, LIST_COLS], U16, name="idx3")
+        q_raw = sb.tile([P, PACK, Q], F32, name="q_raw")
+        q_bf = sb.tile([P, Q, PACK], BF16, name="q_bf", align_bytes=64)
+        q_codes = sb.tile([P, Q], U32, name="q_codes", align_bytes=64)
+        q_plane = sb.tile([P, Q], U8, name="q_plane", align_bytes=64)
+        keys = sb.tile([P, T], U32, name="keys", align_bytes=64)
+        keys_plane = sb.tile([P, T], U8, name="keys_plane", align_bytes=64)
+        notes = sb.tile([P, 2 * U], U8, name="notes", align_bytes=64)
+        notes_plane = sb.tile([P, U], U8, name="notes_plane", align_bytes=64)
+        a = sb.tile([P, T], F32, name="a")
+        b = sb.tile([P, U], F32, name="b")
+        f1 = sb.tile([P, T], F32, name="f1")
+        a2 = sb.tile([P, T], F32, name="a2")
+        b_sel = sb.tile([P, SLOTS], F32, name="b_sel")
+        neg_a_sel = sb.tile([P, SLOTS], F32, name="neg_a_sel")
+        w = sb.tile([P, SLOTS], F32, name="w")
+        a2_sel = sb.tile([P, HALF], F32, name="a2_sel")
+        res = sb.tile([P, SLOTS], F32, name="res")
+
+        nc.vector.memset(notes_plane[:].bitcast(I32), 0)
+        nc.vector.memset(keys_plane[:].bitcast(I32), 0)
+        nc.vector.memset(f1[:], 0.0)
+
+        nc.sync.dma_start(out=q_raw[:], in_=query.rearrange("(p j) q -> p j q", j=PACK))
+        load_scale_rows(nc.scalar, notes_plane, notes_scales)
+        nc.sync.dma_start(out=notes[:].bitcast(I32), in_=notes_words[0].bitcast(I32))
+        nc.sync.dma_start(
+            out=keys[:].bitcast(I32), in_=keys_words[0].rearrange("p n t -> p (n t)").bitcast(I32)
+        )
+        load_scale_rows(nc.sync, keys_plane, keys_scales)
+        nc.sync.dma_start(idx2[:], offs2)
+        nc.sync.dma_start(idx[:], offs)
+        nc.sync.dma_start(idx3[:], offs3)
+
+        q_halves = [slice(0, Q // 2), slice(Q // 2, Q)]
+        for cols in q_halves:
+            nc.vector.tensor_copy(out=q_bf[:, cols, :], in_=q_raw[:, :, cols].rearrange("p j q -> p q j"))
+        for cols in q_halves:
+            nc.vector.quantize_mx(
+                out=q_codes[:, cols].bitcast(FP8X4),
+                scales=q_plane[:, cols],
+                in_=q_bf[:, cols, :].rearrange("p q j -> p (q j)"),
+            )
+
+        def score(name, c, words, plane):
+            bank = psum.tile([P, CHUNK], F32, name=name)
+            nc.tensor.matmul_mx(
+                out=bank[:],
+                lhsT=q_codes[:].bitcast(FP8X4),
+                lhsT_scale=q_plane[:],
+                rhs=words,
+                rhs_scale=plane[:, c * CHUNK : (c + 1) * CHUNK],
+                start=True,
+                stop=True,
+            )
+            return bank
+
+        def empty(c, dst, bank):
+            cols = slice(c * CHUNK, (c + 1) * CHUNK)
+            if c % 2 == 0:
+                nc.scalar.activation(dst[:, cols], bank[:], COPY)
+            else:
+                nc.vector.tensor_copy(dst[:, cols], bank[:])
+
+        lo, hi = slice(0, HALF), slice(HALF, SLOTS)
+        lo_list, hi_list = slice(0, LIST_COLS // 2), slice(LIST_COLS // 2, LIST_COLS)
+
+        b_banks = [
+            score("b%d" % c, c, notes[:, 2 * c * CHUNK : 2 * (c + 1) * CHUNK].bitcast(FP4X4), notes_plane)
+            for c in range(U // CHUNK)
+        ]
+        a_banks = [
+            score("a%d" % c, c, keys[:, c * CHUNK : (c + 1) * CHUNK].bitcast(FP8X4), keys_plane)
+            for c in range(T // CHUNK)
+        ]
+        for c in range(U // CHUNK):
+            empty(c, b, b_banks[c])
+        nc.scalar.activation(b_sel[:, lo], b[:].indirect(idx2[:, lo_list]), COPY)
+        nc.vector.tensor_copy(b_sel[:, hi], b[:].indirect(idx2[:, hi_list]))
+        for c in range(T // CHUNK):
+            empty(c, a, a_banks[c])
+        nc.scalar.activation(neg_a_sel[:, lo], a[:].indirect(idx[:, lo_list]), COPY, scale=-1.0)
+        nc.vector.tensor_scalar(neg_a_sel[:, hi], a[:].indirect(idx[:, hi_list]), -1.0, 0.0, ALU.mult, ALU.add)
+
+        for half in (lo, hi):
+            nc.vector.scalar_tensor_tensor(w[:, half], neg_a_sel[:, half], -1.0, b_sel[:, half], ALU.mult, ALU.max)
+        nc.vector.tensor_tensor(f1[:].indirect(idx[:]), w[:], neg_a_sel[:], ALU.add)
+        nc.vector.tensor_tensor(a2[:], a[:], f1[:], ALU.add)
+
+        nc.scalar.activation(a2_sel[:], a2[:].indirect(idx3[:, hi_list]), COPY)
+        nc.vector.tensor_tensor(res[:, lo], a2[:].indirect(idx3[:, lo_list]), w[:, lo], ALU.subtract)
+        nc.sync.dma_start(out=out[:, lo], in_=res[:, lo])
+        nc.vector.tensor_tensor(res[:, hi], a2_sel[:], w[:, hi], ALU.subtract)
+        nc.scalar.dma_start(out=out[:, hi], in_=res[:, hi])

@@ -20,12 +20,13 @@ P = 128
 PACK = 4
 CHUNK = 256
 HALF = SLOTS // 2
+ADD_SPLIT = 768
 LIST_COLS = SLOTS // 16
 
 
-def load_scale_rows(queue, plane, scales):
+def load_scale_rows(nc, plane, scales):
     for quad in range(4):
-        queue.dma_start(
+        nc.sync.dma_start(
             out=plane[32 * quad : 32 * quad + 4, :].bitcast(I32),
             in_=scales[0, 4 * quad : 4 * quad + 4, :].bitcast(I32),
         )
@@ -46,7 +47,7 @@ def tile_attend_keptbest_two_kernel(
         q_bf = sb.tile([P, Q, PACK], BF16, name="q_bf", align_bytes=64)
         q_codes = sb.tile([P, Q], U32, name="q_codes", align_bytes=64)
         q_plane = sb.tile([P, Q], U8, name="q_plane", align_bytes=64)
-        keys = sb.tile([P, T], U32, name="keys", align_bytes=64)
+        keys = [sb.tile([P, T // 2], U32, name="keys%d" % h, align_bytes=64) for h in range(2)]
         keys_plane = sb.tile([P, T], U8, name="keys_plane", align_bytes=64)
         notes = sb.tile([P, 2 * U], U8, name="notes", align_bytes=64)
         notes_plane = sb.tile([P, U], U8, name="notes_plane", align_bytes=64)
@@ -60,25 +61,26 @@ def tile_attend_keptbest_two_kernel(
         a2_sel = sb.tile([P, HALF], F32, name="a2_sel")
         res = sb.tile([P, SLOTS], F32, name="res")
 
-        nc.vector.memset(notes_plane[:].bitcast(I32), 0)
-        nc.vector.memset(keys_plane[:].bitcast(I32), 0)
         nc.vector.memset(f1[:], 0.0)
 
         nc.sync.dma_start(out=q_raw[:], in_=query.rearrange("(p j) q -> p j q", j=PACK))
-        load_scale_rows(nc.scalar, notes_plane, notes_scales)
+        load_scale_rows(nc, notes_plane, notes_scales)
         nc.sync.dma_start(out=notes[:].bitcast(I32), in_=notes_words[0].bitcast(I32))
-        nc.sync.dma_start(
-            out=keys[:].bitcast(I32), in_=keys_words[0].rearrange("p n t -> p (n t)").bitcast(I32)
-        )
-        load_scale_rows(nc.sync, keys_plane, keys_scales)
+        keys_rows = keys_words[0].rearrange("p n t -> p (n t)").bitcast(I32)
+        nc.sync.dma_start(out=keys[0][:].bitcast(I32), in_=keys_rows[:, : T // 2])
+        load_scale_rows(nc, keys_plane, keys_scales)
+        nc.sync.dma_start(out=keys[1][:].bitcast(I32), in_=keys_rows[:, T // 2 :])
         nc.sync.dma_start(idx2[:], offs2)
         nc.sync.dma_start(idx[:], offs)
         nc.sync.dma_start(idx3[:], offs3)
 
-        q_halves = [slice(0, Q // 2), slice(Q // 2, Q)]
-        for cols in q_halves:
-            nc.vector.tensor_copy(out=q_bf[:, cols, :], in_=q_raw[:, :, cols].rearrange("p j q -> p q j"))
-        for cols in q_halves:
+        def turned(cols):
+            return q_raw[:, :, cols].rearrange("p j q -> p q j")
+
+        nc.vector.tensor_copy(out=q_bf[:, 0:64, :], in_=turned(slice(0, 64)))
+        nc.vector.tensor_copy(out=q_bf[:, 64:96, :], in_=turned(slice(64, 96)))
+        nc.scalar.activation(q_bf[:, 96:128, :], turned(slice(96, 128)), COPY)
+        for cols in (slice(0, Q // 2), slice(Q // 2, Q)):
             nc.vector.quantize_mx(
                 out=q_codes[:, cols].bitcast(FP8X4),
                 scales=q_plane[:, cols],
@@ -98,9 +100,9 @@ def tile_attend_keptbest_two_kernel(
             )
             return bank
 
-        def empty(c, dst, bank):
+        def empty(c, dst, bank, on_scalar):
             cols = slice(c * CHUNK, (c + 1) * CHUNK)
-            if c % 2 == 0:
+            if on_scalar:
                 nc.scalar.activation(dst[:, cols], bank[:], COPY)
             else:
                 nc.vector.tensor_copy(dst[:, cols], bank[:])
@@ -113,25 +115,31 @@ def tile_attend_keptbest_two_kernel(
             for c in range(U // CHUNK)
         ]
         a_banks = [
-            score("a%d" % c, c, keys[:, c * CHUNK : (c + 1) * CHUNK].bitcast(FP8X4), keys_plane)
+            score("a%d" % c, c, keys[c // 2][:, (c % 2) * CHUNK : (c % 2 + 1) * CHUNK].bitcast(FP8X4), keys_plane)
             for c in range(T // CHUNK)
         ]
         for c in range(U // CHUNK):
-            empty(c, b, b_banks[c])
+            empty(c, b, b_banks[c], c % 2 == 0)
         nc.scalar.activation(b_sel[:, lo], b[:].indirect(idx2[:, lo_list]), COPY)
-        nc.vector.tensor_copy(b_sel[:, hi], b[:].indirect(idx2[:, hi_list]))
         for c in range(T // CHUNK):
-            empty(c, a, a_banks[c])
+            empty(c, a, a_banks[c], c == 3)
+        nc.vector.tensor_copy(b_sel[:, hi], b[:].indirect(idx2[:, hi_list]))
         nc.scalar.activation(neg_a_sel[:, lo], a[:].indirect(idx[:, lo_list]), COPY, scale=-1.0)
         nc.vector.tensor_scalar(neg_a_sel[:, hi], a[:].indirect(idx[:, hi_list]), -1.0, 0.0, ALU.mult, ALU.add)
 
         for half in (lo, hi):
             nc.vector.scalar_tensor_tensor(w[:, half], neg_a_sel[:, half], -1.0, b_sel[:, half], ALU.mult, ALU.max)
         nc.vector.tensor_tensor(f1[:].indirect(idx[:]), w[:], neg_a_sel[:], ALU.add)
-        nc.vector.tensor_tensor(a2[:], a[:], f1[:], ALU.add)
+        nc.gpsimd.tensor_tensor(a2[:, ADD_SPLIT:], a[:, ADD_SPLIT:], f1[:, ADD_SPLIT:], ALU.add)
+        for start in range(0, ADD_SPLIT, CHUNK):
+            width = min(CHUNK, ADD_SPLIT - start)
+            cols = slice(start, start + width)
+            nc.vector.tensor_tensor(a2[:, cols], a_banks[start // CHUNK][:, :width], f1[:, cols], ALU.add)
 
         nc.scalar.activation(a2_sel[:], a2[:].indirect(idx3[:, hi_list]), COPY)
         nc.vector.tensor_tensor(res[:, lo], a2[:].indirect(idx3[:, lo_list]), w[:, lo], ALU.subtract)
         nc.sync.dma_start(out=out[:, lo], in_=res[:, lo])
-        nc.vector.tensor_tensor(res[:, hi], a2_sel[:], w[:, hi], ALU.subtract)
-        nc.scalar.dma_start(out=out[:, hi], in_=res[:, hi])
+        for part, queue in ((slice(0, HALF // 2), nc.scalar), (slice(HALF // 2, HALF), nc.sync)):
+            cols = slice(HALF + part.start, HALF + part.stop)
+            nc.vector.tensor_tensor(res[:, cols], a2_sel[:, part], w[:, cols], ALU.subtract)
+            queue.dma_start(out=out[:, cols], in_=res[:, cols])

@@ -20,7 +20,6 @@ P = 128
 PACK = 4
 CHUNK = 256
 HALF = SLOTS // 2
-ADD_SPLIT = 768
 LIST_COLS = SLOTS // 16
 
 
@@ -130,11 +129,7 @@ def tile_attend_keptbest_two_kernel(
         for half in (lo, hi):
             nc.vector.scalar_tensor_tensor(w[:, half], neg_a_sel[:, half], -1.0, b_sel[:, half], ALU.mult, ALU.max)
         nc.vector.tensor_tensor(f1[:].indirect(idx[:]), w[:], neg_a_sel[:], ALU.add)
-        nc.gpsimd.tensor_tensor(a2[:, ADD_SPLIT:], a[:, ADD_SPLIT:], f1[:, ADD_SPLIT:], ALU.add)
-        for start in range(0, ADD_SPLIT, CHUNK):
-            width = min(CHUNK, ADD_SPLIT - start)
-            cols = slice(start, start + width)
-            nc.vector.tensor_tensor(a2[:, cols], a_banks[start // CHUNK][:, :width], f1[:, cols], ALU.add)
+        nc.vector.tensor_tensor(a2[:], a[:], f1[:], ALU.add)
 
         nc.scalar.activation(a2_sel[:], a2[:].indirect(idx3[:, hi_list]), COPY)
         nc.vector.tensor_tensor(res[:, lo], a2[:].indirect(idx3[:, lo_list]), w[:, lo], ALU.subtract)

from contextlib import ExitStack

import concourse.mybir as mybir

D, T, U, SLOTS, Q = 512, 1024, 1024, 512, 128
FLOPS = 2 * D * Q * (T + U)

F32 = mybir.dt.float32
BF16 = mybir.dt.bfloat16
I32 = mybir.dt.int32
U32 = mybir.dt.uint32
U16 = mybir.dt.uint16
U8 = mybir.dt.uint8
FP8X4 = mybir.dt.float8_e4m3fn_x4
FP4X4 = mybir.dt.float4_e2m1fn_x4
ALU = mybir.AluOpType
COPY = mybir.ActivationFunctionType.Copy

P = 128
PACK = 4
CHUNK = 256
HALF = SLOTS // 2
LIST_COLS = SLOTS // 16


def load_scale_rows(nc, plane, scales):
    for quad in range(4):
        nc.sync.dma_start(
            out=plane[32 * quad : 32 * quad + 4, :].bitcast(I32),
            in_=scales[0, 4 * quad : 4 * quad + 4, :].bitcast(I32),
        )


def tile_attend_keptbest_two_kernel(
    tc, query, keys_words, keys_scales, notes_words, notes_scales, offs, offs2, offs3, out
):
    nc = tc.nc
    with ExitStack() as ctx:
        sb = ctx.enter_context(tc.tile_pool(name="sb", bufs=1))
        psum = ctx.enter_context(tc.psum_pool(name="psum", bufs=1))

        idx = sb.tile([P, LIST_COLS], U16, name="idx")
        idx2 = sb.tile([P, LIST_COLS], U16, name="idx2")
        idx3 = sb.tile([P, LIST_COLS], U16, name="idx3")
        q_raw = sb.tile([P, PACK, Q], F32, name="q_raw")
        q_bf = sb.tile([P, Q, PACK], BF16, name="q_bf", align_bytes=64)
        q_codes = sb.tile([P, Q], U32, name="q_codes", align_bytes=64)
        q_plane = sb.tile([P, Q], U8, name="q_plane", align_bytes=64)
        keys = [sb.tile([P, T // 2], U32, name="keys%d" % h, align_bytes=64) for h in range(2)]
        keys_plane = sb.tile([P, T], U8, name="keys_plane", align_bytes=64)
        notes = sb.tile([P, 2 * U], U8, name="notes", align_bytes=64)
        notes_plane = sb.tile([P, U], U8, name="notes_plane", align_bytes=64)
        a = sb.tile([P, T], F32, name="a")
        b = sb.tile([P, U], F32, name="b")
        f1 = sb.tile([P, T], F32, name="f1")
        a2 = sb.tile([P, T], F32, name="a2")
        b_sel = sb.tile([P, SLOTS], F32, name="b_sel")
        neg_a_sel = sb.tile([P, SLOTS], F32, name="neg_a_sel")
        w = sb.tile([P, SLOTS], F32, name="w")
        a2_sel = sb.tile([P, HALF], F32, name="a2_sel")
        res = sb.tile([P, SLOTS], F32, name="res")

        nc.vector.memset(f1[:], 0.0)

        nc.sync.dma_start(out=q_raw[:], in_=query.rearrange("(p j) q -> p j q", j=PACK))
        load_scale_rows(nc, notes_plane, notes_scales)
        nc.sync.dma_start(out=notes[:].bitcast(I32), in_=notes_words[0].bitcast(I32))
        keys_rows = keys_words[0].rearrange("p n t -> p (n t)").bitcast(I32)
        nc.sync.dma_start(out=keys[0][:].bitcast(I32), in_=keys_rows[:, : T // 2])
        load_scale_rows(nc, keys_plane, keys_scales)
        nc.sync.dma_start(out=keys[1][:].bitcast(I32), in_=keys_rows[:, T // 2 :])
        nc.sync.dma_start(idx2[:], offs2)
        nc.sync.dma_start(idx[:], offs)
        nc.sync.dma_start(idx3[:], offs3)

        def turned(cols):
            return q_raw[:, :, cols].rearrange("p j q -> p q j")

        nc.vector.tensor_copy(out=q_bf[:, 0:64, :], in_=turned(slice(0, 64)))
        nc.vector.tensor_copy(out=q_bf[:, 64:96, :], in_=turned(slice(64, 96)))
        nc.scalar.activation(q_bf[:, 96:128, :], turned(slice(96, 128)), COPY)
        for cols in (slice(0, Q // 2), slice(Q // 2, Q)):
            nc.vector.quantize_mx(
                out=q_codes[:, cols].bitcast(FP8X4),
                scales=q_plane[:, cols],
                in_=q_bf[:, cols, :].rearrange("p q j -> p (q j)"),
            )

        def score(name, c, words, plane):
            bank = psum.tile([P, CHUNK], F32, name=name)
            nc.tensor.matmul_mx(
                out=bank[:],
                lhsT=q_codes[:].bitcast(FP8X4),
                lhsT_scale=q_plane[:],
                rhs=words,
                rhs_scale=plane[:, c * CHUNK : (c + 1) * CHUNK],
                start=True,
                stop=True,
            )
            return bank

        def empty(c, dst, bank, on_scalar):
            cols = slice(c * CHUNK, (c + 1) * CHUNK)
            if on_scalar:
                nc.scalar.activation(dst[:, cols], bank[:], COPY)
            else:
                nc.vector.tensor_copy(dst[:, cols], bank[:])

        lo, hi = slice(0, HALF), slice(HALF, SLOTS)
        lo_list, hi_list = slice(0, LIST_COLS // 2), slice(LIST_COLS // 2, LIST_COLS)

        b_banks = [
            score("b%d" % c, c, notes[:, 2 * c * CHUNK : 2 * (c + 1) * CHUNK].bitcast(FP4X4), notes_plane)
            for c in range(U // CHUNK)
        ]
        a_banks = [
            score("a%d" % c, c, keys[c // 2][:, (c % 2) * CHUNK : (c % 2 + 1) * CHUNK].bitcast(FP8X4), keys_plane)
            for c in range(T // CHUNK)
        ]
        for c in range(U // CHUNK):
            empty(c, b, b_banks[c], c % 2 == 0)
        nc.scalar.activation(b_sel[:, lo], b[:].indirect(idx2[:, lo_list]), COPY)
        for c in range(T // CHUNK):
            empty(c, a, a_banks[c], c == 3)
        nc.vector.tensor_copy(b_sel[:, hi], b[:].indirect(idx2[:, hi_list]))
        nc.scalar.activation(neg_a_sel[:, lo], a[:].indirect(idx[:, lo_list]), COPY, scale=-1.0)
        nc.vector.tensor_scalar(neg_a_sel[:, hi], a[:].indirect(idx[:, hi_list]), -1.0, 0.0, ALU.mult, ALU.add)

        for half in (lo, hi):
            nc.vector.scalar_tensor_tensor(w[:, half], neg_a_sel[:, half], -1.0, b_sel[:, half], ALU.mult, ALU.max)
        nc.vector.tensor_tensor(f1[:].indirect(idx[:]), w[:], neg_a_sel[:], ALU.add)
        nc.vector.tensor_tensor(a2[:], a[:], f1[:], ALU.add)

        nc.scalar.activation(a2_sel[:], a2[:].indirect(idx3[:, hi_list]), COPY)
        nc.vector.tensor_tensor(res[:, lo], a2[:].indirect(idx3[:, lo_list]), w[:, lo], ALU.subtract)
        nc.sync.dma_start(out=out[:, lo], in_=res[:, lo])
        for part, queue in ((slice(0, HALF // 2), nc.scalar), (slice(HALF // 2, HALF), nc.sync)):
            cols = slice(HALF + part.start, HALF + part.stop)
            nc.vector.tensor_tensor(res[:, cols], a2_sel[:, part], w[:, cols], ALU.subtract)
            queue.dma_start(out=out[:, cols], in_=res[:, cols])
